import numpy as np, ml_dtypes
CORES = [32,40,48,56,64,72,80,88,96,104,112,120]
N = 12
QP = 128
def setup_inputs(rng):
    return {"q": rng.standard_normal((N, 128, QP), dtype=np.float32).astype(ml_dtypes.bfloat16), "k": rng.standard_normal((N, 128, 128), dtype=np.float32).astype(ml_dtypes.bfloat16), "v": rng.standard_normal((N, 128, 128), dtype=np.float32).astype(ml_dtypes.bfloat16), "b": (8 * rng.standard_normal((N, 128, N * QP), dtype=np.float32)).astype(ml_dtypes.bfloat16)}
def setup_inputs_big(rng):
    d = setup_inputs(rng)
    for k in ("q", "k", "v", "b"): d[k] = (d[k].astype(np.float32) * 1024.0).astype(d[k].dtype)
    return d
def setup_inputs_small(rng):
    d = setup_inputs(rng)
    for k in ("q", "k", "v", "b"): d[k] = (d[k].astype(np.float32) * (1 / 1024.0)).astype(d[k].dtype)
    return d
def setup_inputs_apart(rng):
    d = setup_inputs(rng)
    f = (10.0 ** rng.permutation(np.linspace(-1.5, 1.5, N))).astype(np.float32).reshape(N, 1, 1)
    for k in ("q", "k", "v", "b"): d[k] = (d[k].astype(np.float32) * f).astype(d[k].dtype)
    return d
def reference(q, k, v, b):
    Q, K, V, B = q.astype(np.float64), k.astype(np.float64), v.astype(np.float64), b.astype(np.float64)
    y = np.zeros((N, 128, QP))
    for r in range(N):
        for j in range(N):
            y[r] += V[j].T @ np.maximum(K[j].T @ Q[r] + B[r][:, QP * j:QP * j + QP], 0.0)
    return {"y": y.astype(ml_dtypes.bfloat16 if q.dtype != np.float64 else np.float64)}

from concourse.bass import DstId, RemoteDMATransfer
from concourse.mybir import AluOpType

N = 12
P = 128
W = 2 * P
NBANK = 6

HELPERS = (
    ("near_gate", 0, (("O", 3), ("O", 4))),
    ("far_gate", 0, (("O", 1), ("O", 2))),
    ("near_gate", 1, (("O", 0),)),
    ("far_gate", 1, (("O", 5),)),
    ("near_plain", 0, (("S", 4), ("S", 5))),
)
COPY_CALLS = ((0, 1), (2, 3, 4))
DIRECT = (("S", 1), ("S", 2), ("S", 3))
ENG_COPY = 8
ENG_OUT = 8
T_COPY = 0.25
T_HOP = 4.0

SCRATCH = {
    "KV": ("sbuf", [P, N * W], "bfloat16"),
    "D": ("dram", [P, W], "bfloat16"),
    "Q": ("sbuf", [P, P], "bfloat16"),
    "NQ": ("sbuf", [P, P], "bfloat16"),
    "ZERO": ("sbuf", [P, P], "bfloat16"),
    "BT": ("sbuf", [P, N * P], "bfloat16"),
    "M": ("sbuf", [P, N * P], "bfloat16"),
    "ASB": ("sbuf", [P, P], "float32"),
    "YSB": ("sbuf", [P, P], "bfloat16"),
    "PA": ("psum", [P, 512], "float32"),
    "PB": ("psum", [P, 512], "float32"),
}
for _i in range(NBANK):
    SCRATCH["PX%d" % _i] = ("psum", [P, 512], "float32")

SEMAPHORES = (["ldkv", "ldd", "ldq", "ldb", "zs", "nqs", "asum", "bsum", "cs", "ys", "st", "sent"]
              + ["arr%d" % _j for _j in range(N)]
              + ["xs%d" % _j for _j in range(N)]
              + ["ms%d" % _j for _j in range(N)])


def _layout(T, topo):
    cores = list(T.cores)
    n = len(cores)
    every = range(topo.CHIPS * topo.CORES_PER_CHIP)
    out = []
    for a in range(n):
        c0 = cores[a]
        ch = topo.chip(c0)
        plane = [j for j in range(n) if j == a or topo.same_plane(ch, topo.chip(cores[j]))]
        other = [j for j in range(n) if j not in plane]
        p = plane.index(a)
        pm = [i for i, j in enumerate(other) if topo.mates(ch, topo.chip(cores[j]))][0]
        ring = {"S": [plane[(p + d) % len(plane)] for d in range(len(plane))],
                "O": [other[(pm + d) % len(other)] for d in range(len(other))]}
        local = [c for c in every if topo.chip(c) == ch and T.rank_of(c) is None]
        gate = [c for c in local if topo.may_write(c, cores[other[0]])]
        near = [c for c in local if topo.die(c) == topo.die(c0)]
        kinds = {"near_gate": [c for c in gate if c in near],
                 "far_gate": [c for c in gate if c not in near],
                 "near_plain": [c for c in near if c not in gate],
                 "far_plain": [c for c in local if c not in near and c not in gate]}
        helpers = [(kinds[kind][idx], [ring[t][d] for t, d in places], (i + 1) * T_COPY + T_HOP)
                   for i, (kind, idx, places) in enumerate(HELPERS)]
        out.append({"helpers": helpers, "direct": [ring[t][d] for t, d in DIRECT],
                    "t_direct": len(HELPERS) * T_COPY})
    return out


def _pick(allowed, n, spare=0):
    m, got = 0, 0
    for pool in (allowed & ~spare, allowed & spare):
        e = 0
        while got < n and (pool >> e):
            if (pool >> e) & 1:
                m |= 1 << e
                got += 1
            e += 1
    return m


def _write(g, T, topo, me, a, src, dst, dests, want, spare=0):
    allowed = topo.mask(me, dests[0])
    for d in dests[1:]:
        allowed &= topo.mask(me, d)
    ids = [DstId(rid=topo.addr(d)[0], pnc=topo.addr(d)[1]) for d in dests]
    g.remote_dma_fused([RemoteDMATransfer(dst_ids=ids, dma_engine_mask=_pick(allowed, want, spare),
                                          remote_sem=T.sem["arr%d" % a], srcs=[src],
                                          dsts=[dst for _ in dests], alu_op=0)], local_sem=T.sem.sent)
    return want


def _helper(g, core, T, topo, lay):
    cores = list(T.cores)
    for a in range(len(cores)):
        for h, ranks, _t in lay[a]["helpers"]:
            if h != core:
                continue
            g.wait_ge(T.sem["arr%d" % a], ENG_COPY)
            n = _write(g, T, topo, core, a, T.D[:], T.KV[:, a * W:(a + 1) * W], [cores[j] for j in ranks], ENG_OUT)
            g.wait_ge(T.sem.sent, n)


def rank_program(g, core, T, topo):
    lay = _layout(T, topo)
    r = T.rank_of(core)
    if r is None:
        _helper(g, core, T, topo, lay)
        return
    cores = list(T.cores)
    sem = T.sem
    mine = T.KV[:, r * W:(r + 1) * W]

    g.sync.dma_start(T.D[:, 0:P], T.k[:]).then_inc(sem.ldd, 16)
    g.scalar.dma_start(T.D[:, P:W], T.v[:]).then_inc(sem.ldd, 16)
    g.sync.dma_start(T.Q[:], T.q[:]).then_inc(sem.ldq, 16)
    g.scalar.dma_start(T.KV[:, r * W:r * W + P], T.k[:]).then_inc(sem.ldkv, 16)
    g.sync.dma_start(T.KV[:, r * W + P:(r + 1) * W], T.v[:]).then_inc(sem.ldkv, 16)
    half = (N // 2) * P
    g.scalar.dma_start(T.BT[:, 0:half], T.b[:, 0:half]).then_inc(sem.ldb, 16)
    g.sync.dma_start(T.BT[:, half:N * P], T.b[:, half:N * P]).then_inc(sem.ldb, 16)

    left = 0
    direct = [cores[j] for j in lay[r]["direct"]]
    leaving = topo.mask(core, direct[0])
    g.wait_ge(sem.ldd, 32)
    for group in COPY_CALLS:
        left += _write(g, T, topo, core, r, T.D[:], T.D[:], [lay[r]["helpers"][i][0] for i in group],
                       ENG_COPY, spare=leaving)
    left += _write(g, T, topo, core, r, T.D[:], mine, direct, ENG_OUT)

    due = []
    for a in range(N):
        for i, j in enumerate(lay[a]["direct"]):
            if j == r:
                due.append((lay[a]["t_direct"] + i + 1, a))
        for _h, ranks, t in lay[a]["helpers"]:
            for i, j in enumerate(ranks):
                if j == r:
                    due.append((t + i + 1, a))
    order = [r] + [a for _t, a in sorted(due)]

    def kk(j):
        return T.KV[:, j * W:j * W + P]

    def vv(j):
        return T.KV[:, j * W + P:(j + 1) * W]

    def bb(j):
        return T.BT[:, j * P:(j + 1) * P]

    def mm(j):
        return T.M[:, j * P:(j + 1) * P]

    def px(i):
        return T["PX%d" % (i % NBANK)][:, 0:P]

    te = g.tensor
    te.wait_ge(sem.nqs, 1)
    te.wait_ge(sem.ldb, 32)
    for i, j in enumerate(order):
        if j == r:
            te.wait_ge(sem.ldkv, 32)
        else:
            te.wait_ge(sem["arr%d" % j], ENG_OUT)
        te.matmul(px(i), kk(j), T.NQ[:], start=True, stop=True).then_inc(sem["xs%d" % j], 1)
        te.matmul(T.PA[:, 0:P], vv(j), bb(j), start=(i == 0), stop=(i == N - 1)).then_inc(sem.asum, 1)
        if i > 0:
            jp = order[i - 1]
            te.wait_ge(sem["ms%d" % jp], 1)
            te.matmul(T.PB[:, 0:P], vv(jp), mm(jp), start=(i == 1), stop=False).then_inc(sem.bsum, 1)
    jl = order[N - 1]
    te.wait_ge(sem["ms%d" % jl], 1)
    te.matmul(T.PB[:, 0:P], vv(jl), mm(jl), start=False, stop=True).then_inc(sem.bsum, 1)

    ve = g.vector
    ve.memset(T.ZERO[:], 0.0).then_inc(sem.zs, 1)
    ve.wait_ge(sem.zs, 1)
    ve.wait_ge(sem.ldq, 16)
    ve.tensor_tensor(T.NQ[:], T.ZERO[:], T.Q[:], AluOpType.subtract).then_inc(sem.nqs, 1)
    ve.wait_ge(sem.ldb, 32)
    for i, j in enumerate(order):
        ve.wait_ge(sem["xs%d" % j], 1)
        ve.tensor_tensor(mm(j), px(i), bb(j), AluOpType.min).then_inc(sem["ms%d" % j], 1)
    ve.wait_ge(sem.asum, N)
    ve.tensor_copy(T.ASB[:], T.PA[:, 0:P]).then_inc(sem.cs, 1)
    ve.wait_ge(sem.cs, 1)
    ve.wait_ge(sem.bsum, N)
    ve.tensor_tensor(T.YSB[:], T.ASB[:], T.PB[:, 0:P], AluOpType.subtract).then_inc(sem.ys, 1)

    g.sync.wait_ge(sem.ys, 1)
    g.sync.dma_start(T.y[:], T.YSB[:]).then_inc(sem.st, 16)
    g.sync.wait_ge(sem.st, 16)
    g.wait_ge(sem.sent, left)
